import numpy as np
import ml_dtypes


def mxq(x, axis, fmt="e4m3"):
    dtype, down = {"e4m3": (ml_dtypes.float8_e4m3fn, 7), "e5m2": (ml_dtypes.float8_e5m2, 14)}[fmt]
    v = np.moveaxis(np.asarray(x, np.float32).astype(ml_dtypes.bfloat16).astype(np.float64), axis, -1)
    blocks = v.reshape(v.shape[:-1] + (-1, 32))
    amax = np.abs(blocks).max(-1, keepdims=True)
    byte = np.maximum(np.where(amax > 0, np.frexp(amax)[1] - 1 + 127, 0) - down, 1)
    scale = np.exp2(byte - 127.0)
    codes = (blocks / scale).astype(np.float32).astype(dtype).astype(np.float64)
    return np.moveaxis((codes * scale).reshape(v.shape), -1, axis)


WIDE = False


def mx_kscale(k):
    if not WIDE:
        return np.ones(k)
    levels = np.array([10, -10, 5, -5, 0])
    if k % 512:
        return np.exp2(np.random.permutation(np.resize(levels, k // 32))).repeat(32)
    a = np.empty((k // 512, 16))
    for p in range(k // 512):
        a[p, :8] = np.random.permutation(np.resize(levels, 8))
        for g in range(8):
            far = levels[np.abs(levels - a[p, g]) >= 10]
            a[p, g + 8] = far[np.random.randint(len(far))]
    return np.exp2(a.ravel()).repeat(32)


def f64(x):
    return np.asarray(x).astype(np.float64)


def striped(idx):
    return np.tile(np.asarray(idx).reshape(-1, 16).T, (8, 1)).astype(np.uint16)


def unstriped(offs):
    return offs[:16].T.reshape(-1).astype(np.int64)


E2M1 = np.array([0.0, 0.5, 1.0, 1.5, 2.0, 3.0, 4.0, 6.0, -0.0, -0.5, -1.0, -1.5, -2.0, -3.0, -4.0, -6.0])


def pack_weight(w, fmt):
    k, n = w.shape
    w = f64(np.asarray(w, np.float32).astype(ml_dtypes.bfloat16)).reshape(k // 32, 32, n)
    amax = np.abs(w).max(1)
    if fmt == "e4m3":
        byte = np.frexp(amax)[1] - 1 + 127 - 7
    else:
        mant, ex = np.frexp(amax / 6.0)
        byte = np.where(mant > 0.5, ex, ex - 1) + 127
    byte = np.clip(np.where(amax > 0, byte, 1), 1, 254)
    scaled = (w * np.exp2(127.0 - byte)[:, None, :]).reshape(k, n).astype(np.float32)
    by_word = np.ascontiguousarray(scaled.reshape(k // 512, 128, 4, n).transpose(0, 1, 3, 2))
    if fmt == "e4m3":
        words = by_word.astype(ml_dtypes.float8_e4m3fn).view(np.uint8)
    else:
        c = by_word.astype(ml_dtypes.float4_e2m1fn).view(np.uint8) & 0xF
        words = (c[..., 0::2] | (c[..., 1::2] << 4)).reshape(k // 512, 128, 2 * n)
    return np.ascontiguousarray(words), np.ascontiguousarray(byte.astype(np.uint8).reshape(k // 512, 16, n))


def unpack_weight(words, scales, fmt):
    g, _, n = scales.shape
    words = np.ascontiguousarray(words).reshape(g, 128, n, -1)
    if fmt == "e4m3":
        vals = words.view(ml_dtypes.float8_e4m3fn).astype(np.float64)
    else:
        nib = np.empty((g, 128, n, 4), np.uint8)
        nib[..., 0::2] = words & 0xF
        nib[..., 1::2] = words >> 4
        vals = E2M1[nib]
    vals = vals * np.repeat(np.exp2(scales.astype(np.float64) - 127.0), 8, axis=1)[..., None]
    return vals.transpose(0, 1, 3, 2).reshape(g * 512, n)


K, R, F, T, J, M = 512, 128, 512, 2048, 512, 256


def setup_inputs():
    n = np.random.standard_normal
    idx = np.random.permutation(T)[:J]
    idx2 = np.random.permutation(J)[:M]
    idx3 = np.random.permutation(J)[:M]
    fk = mx_kscale(K)
    ff = mx_kscale(F)
    fj = mx_kscale(J)
    tj = np.ones(T)
    tj[idx] = fj
    tabp = pack_weight(n((K, T)) / fk[:, None], "e2m1")
    return {
        "tab_words": tabp[0],
        "tab_scales": tabp[1],
        "w1": (n((K, R)) * 1 / np.sqrt(K) * fk[:, None]).astype(np.float32),
        "reserve": (np.random.uniform(0.3, 1.5, (R, 1))).astype(np.float32),
        "wo": (n((F, R)) * 1 / np.sqrt(F) * ff[:, None]).astype(np.float32),
        "dy": (n((F, M)) / ff[:, None]).astype(np.float32),
        "js": (np.random.uniform(0.5, 2.0, (1, J)) * fj).astype(np.float32),
        "xrows": (n((K, T)) / tj).astype(np.float32),
        "old": (n((K, R)) * 4.0).astype(np.float32),
        "offs": striped(idx),
        "offs2": striped(idx2),
        "offs3": striped(idx3),
    }


def reference(tab_words, tab_scales, w1, reserve, wo, dy, js, xrows, old, offs, offs2, offs3):
    idx = unstriped(offs)
    idx2 = unstriped(offs2)
    idx3 = unstriped(offs3)
    tabu = unpack_weight(tab_words, tab_scales, "e2m1")
    w1q = mxq(f64(w1), 0, "e4m3")
    tabidxg = tabu[:, idx]
    a = w1q.T @ tabidxg
    h1 = np.exp(a)
    woq = mxq(f64(wo), 0, "e4m3")
    dyq = mxq(f64(dy), 0, "e4m3")
    c0 = woq.T @ dyq
    e1 = c0 / (h1[:, idx2] + h1[:, idx3] + f64(reserve))
    s1 = np.zeros((R, J))
    s1[:, idx2] = e1
    e2 = c0 * h1[:, idx2] / np.square(h1[:, idx2] + h1[:, idx3] + f64(reserve)) * (-1.0)
    s2 = np.zeros((R, J))
    s2[:, idx2] = e2
    e3 = c0 * h1[:, idx2] / np.square(h1[:, idx2] + h1[:, idx3] + f64(reserve)) * (-1.0)
    s3 = np.zeros((R, J))
    s3[:, idx3] = e3
    dh1 = s1 + s2 + s3
    da = dh1 * h1
    gs = da * f64(js)
    gt1 = gs.T
    xt = f64(xrows)[:, idx].T
    xtq = mxq(xt, 0, "e4m3")
    gt1q = mxq(gt1, 0, "e4m3")
    gw = xtq.T @ gt1q
    y = gw + f64(old)
    return y

@@ -1,0 +1,187 @@
+from contextlib import ExitStack
+
+import concourse.mybir as mybir
+from concourse.masks import make_identity
+
+K, R, F, T, J, M = 512, 128, 512, 2048, 512, 256
+FLOPS = 2 * K * R * J + 2 * F * R * M + 2 * J * K * R
+
+F32 = mybir.dt.float32
+BF16 = mybir.dt.bfloat16
+I32 = mybir.dt.int32
+U32 = mybir.dt.uint32
+U16 = mybir.dt.uint16
+U8 = mybir.dt.uint8
+FP8X4 = mybir.dt.float8_e4m3fn_x4
+FP4X4 = mybir.dt.float4_e2m1fn_x4
+ALU = mybir.AluOpType
+ACT = mybir.ActivationFunctionType
+
+P = 128
+PACK = 4
+
+
+def tile_attend_cratiopairs_w_kernel(tc, tab_words, tab_scales, w1, reserve, wo, dy, js, xrows, old,
+                                      offs, offs2, offs3, out):
+    nc = tc.nc
+    with ExitStack() as ctx:
+        sb = ctx.enter_context(tc.tile_pool(name="sb", bufs=1))
+        ps = ctx.enter_context(tc.psum_pool(name="ps", bufs=1))
+
+        def tile(name, shape, dtype, over=None):
+            return sb.tile(shape, dtype, name=name, tag=over or name, align_bytes=64)
+
+        slots = sb.tile([P, J // 16], U16, name="slots")
+        firsts = sb.tile([P, M // 16], U16, name="firsts")
+        seconds = sb.tile([P, M // 16], U16, name="seconds")
+        words = tile("words", [P, T], U16)
+        planes = tile("planes", [P, T], U8)
+        w1_raw = tile("w1_raw", [P, PACK, R], F32)
+        wo_raw = tile("wo_raw", [P, PACK, R], F32)
+        dy_raw = tile("dy_raw", [P, PACK, M], F32)
+        x_raw = [tile("x_raw%d" % i, [P, T], F32) for i in range(PACK)]
+        old_sb = tile("old_sb", [P, PACK * R], F32)
+        res = tile("res", [P, 1], F32)
+        js_sb = tile("js_sb", [P, PACK], F32)
+        ident = tile("ident", [P, P], F32)
+        placed_a = tile("placed_a", [P, J], F32)
+        placed_b = tile("placed_b", [P, J], F32)
+
+        nc.vector.memset(planes[:].bitcast(I32), 0)
+        nc.sync.dma_start(slots[:], offs)
+        nc.sync.dma_start(firsts[:], offs2)
+        nc.sync.dma_start(words[:].bitcast(I32), tab_words[0].bitcast(I32))
+        nc.sync.dma_start(w1_raw[:], w1.rearrange("(p t) r -> p t r", t=PACK))
+        scale_rows = tab_scales[0].bitcast(I32)
+        for q in range(4):
+            nc.sync.dma_start(planes[32 * q:32 * q + 4, :].bitcast(I32), scale_rows[4 * q:4 * q + 4, :])
+        nc.sync.dma_start(wo_raw[:], wo.rearrange("(p t) r -> p t r", t=PACK))
+        nc.sync.dma_start(dy_raw[:], dy.rearrange("(p t) m -> p t m", t=PACK))
+        nc.sync.dma_start(seconds[:], offs3)
+        x_blocks = xrows.rearrange("(p i) t -> i p t", i=PACK)
+        for i in range(PACK):
+            nc.sync.dma_start(x_raw[i][:], x_blocks[i])
+        nc.sync.dma_start(old_sb[:], old.rearrange("(p i) r -> p (i r)", i=PACK))
+        make_identity(nc, ident[:])
+        nc.gpsimd.dma_start(res[:], reserve)
+        nc.gpsimd.dma_start(js_sb[:], js.rearrange("o (p t) -> p (o t)", t=PACK))
+        nc.vector.memset(placed_a[:], 0.0)
+        nc.vector.memset(placed_b[:], 0.0)
+        neg_res = tile("neg_res", [P, 1], F32)
+        nc.gpsimd.tensor_scalar(neg_res[:], res[:], -1.0, 0.0, ALU.mult, ALU.add)
+
+        def quantise(name, grouped, width, over=None):
+            codes = tile(name + "_codes", [P, width], U32)
+            scales = tile(name + "_scales", [P, width], U8, over)
+            nc.vector.quantize_mx(out=codes[:].bitcast(FP8X4), scales=scales[:], in_=grouped)
+            return codes, scales
+
+        tab_codes = tile("tab_codes", [P, J], U16)
+        tab_planes = tile("tab_planes", [P, J], U8)
+        w1_il = tile("w1_il", [P, R, PACK], BF16)
+        wo_il = tile("wo_il", [P, R, PACK], BF16)
+        dy_il = tile("dy_il", [P, M, PACK], BF16)
+        nc.scalar.copy(w1_il[:], w1_raw[:].rearrange("p t r -> p r t"))
+        nc.scalar.copy(wo_il[:], wo_raw[:].rearrange("p t r -> p r t"))
+        nc.vector.tensor_copy(tab_codes[:], words[:].indirect(slots[:]))
+        nc.vector.tensor_copy(tab_planes[:], planes[:].indirect(slots[:]))
+        w1_codes, w1_scales = quantise("w1", w1_il[:].rearrange("p r t -> p (r t)"), R)
+        h1 = tile("h1", [P, J], F32)
+        for half in range(2):
+            cols = slice(half * J // 2, (half + 1) * J // 2)
+            a_ps = ps.tile([P, J // 2], F32, name="a_ps%d" % half)
+            nc.tensor.matmul_mx(out=a_ps[:], lhsT=w1_codes[:].bitcast(FP8X4), lhsT_scale=w1_scales[:],
+                                rhs=tab_codes[:, cols].bitcast(FP4X4), rhs_scale=tab_planes[:, cols],
+                                start=True, stop=True)
+            nc.scalar.activation(h1[:, cols], a_ps[:], ACT.Exp)
+
+        nc.vector.tensor_copy(dy_il[:], dy_raw[:].rearrange("p t m -> p m t"))
+        wo_codes, wo_scales = quantise("wo", wo_il[:].rearrange("p r t -> p (r t)"), R)
+        dy_codes, dy_scales = quantise("dy", dy_il[:].rearrange("p m t -> p (m t)"), M)
+        c0_ps = ps.tile([P, M], F32, name="c0_ps")
+        nc.tensor.matmul_mx(out=c0_ps[:], lhsT=wo_codes[:].bitcast(FP8X4), lhsT_scale=wo_scales[:],
+                            rhs=dy_codes[:].bitcast(FP8X4), rhs_scale=dy_scales[:], start=True, stop=True)
+
+        x_il = [tile("x_il%d" % half, [P, 2, P, PACK], BF16) for half in range(2)]
+
+        def gather_x(i, over):
+            picked = tile("x_picked%d" % i, [P, J], BF16, over)
+            nc.vector.tensor_copy(picked[:], x_raw[i][:].indirect(slots[:]))
+            return picked
+
+        def gather_x_on_scalar(i, over):
+            narrow = tile("x_narrow%d" % i, [P, T], BF16, over)
+            nc.scalar.activation(narrow[:], x_raw[i][:], ACT.Copy)
+            picked = tile("x_picked%d" % i, [P, J], BF16)
+            nc.scalar.activation(picked[:], narrow[:].indirect(slots[:]), ACT.Copy)
+            return picked
+
+        def turn_x(i, picked):
+            pairs = picked[:].bitcast(F32)
+            turned = ps.tile([P, 2, P], F32, name="x_turned%d" % (i % 2), tag="x_turned%d" % (i % 2))
+            for u in range(2):
+                nc.tensor.transpose(turned[:, u, :], pairs[:, u:J // 2:2], ident[:])
+            nc.scalar.copy(x_il[i // 2][:, i % 2].bitcast(F32), turned[:].rearrange("p u k -> p k u"))
+
+        def quantise_x(half, over=None):
+            return quantise("x%d" % half, x_il[half][:].rearrange("p i k t -> p (i k t)"), 2 * P, over)
+
+        root = tile("root", [P, M], F32)
+        nc.scalar.activation(root[:, 0:1], h1[:, J - 1:J], ACT.Abs_reciprocal_sqrt)
+        h_a = tile("h_a", [P, M], F32)
+        h_b = tile("h_b", [P, M], F32)
+        h_sum = tile("h_sum", [P, M], F32)
+        top = tile("top", [P, M], F32)
+        nc.vector.tensor_copy(h_a[:], h1[:].indirect(firsts[:]))
+        nc.vector.tensor_copy(h_b[:], h1[:].indirect(seconds[:]))
+        nc.vector.tensor_tensor(h_sum[:], h_a[:], h_b[:], ALU.add)
+        nc.vector.tensor_tensor(top[:], c0_ps[:], h_a[:], ALU.mult)
+
+        inv = tile("inv", [P, M], F32)
+        nc.scalar.activation(root[:], h_sum[:], ACT.Abs_reciprocal_sqrt, bias=res[:])
+        nc.scalar.activation(inv[:], root[:], ACT.Square)
+        neg_rest = tile("neg_rest", [P, M], F32, "h_sum")
+        nc.scalar.activation(neg_rest[:], h_b[:], ACT.Identity, bias=neg_res[:], scale=-1.0)
+
+        turn_x(0, gather_x(0, "h1"))
+        picked1 = gather_x_on_scalar(1, "root")
+
+        share = tile("share", [P, M], F32, "x_raw0")
+        e2 = tile("e2", [P, M], F32)
+        nc.vector.tensor_tensor(share[:], top[:], inv[:], ALU.mult)
+        nc.vector.scalar_tensor_tensor(e2[:], share[:], -1.0, inv[:], ALU.mult, ALU.mult)
+        nc.vector.tensor_tensor(placed_b[:].indirect(seconds[:]), e2[:], h_b[:], ALU.mult)
+        nc.vector.tensor_tensor(placed_a[:].indirect(firsts[:]), e2[:], neg_rest[:], ALU.mult)
+
+        da_ps = ps.tile([P, PACK, R], F32, name="da_ps")
+
+        def turn_placed(placed, first, last):
+            for t in range(PACK):
+                nc.tensor.matmul(da_ps[:, t, :], lhsT=placed[:, t:J:PACK], rhs=ident[:], is_transpose=True,
+                                 start=(first and t == 0), stop=(last and t == PACK - 1))
+
+        turn_placed(placed_b, True, False)
+        turn_x(1, picked1)
+        turn_placed(placed_a, False, True)
+        turn_x(2, gather_x(2, "h_b"))
+        turn_x(3, gather_x(3, "h_sum"))
+        g_il = tile("g_il", [P, R, PACK], BF16, "x_raw3")
+        nc.vector.tensor_tensor(g_il[:], da_ps[:].rearrange("p t r -> p r t"),
+                                js_sb[:].unsqueeze(1).to_broadcast([P, R, PACK]), ALU.mult)
+        xq = [quantise_x(0, "js_sb")]
+        g_codes, g_scales = quantise("g", g_il[:].rearrange("p r t -> p (r t)"), R)
+        xq.append(quantise_x(1))
+
+        out_rows = out.rearrange("(p i) r -> p (i r)", i=PACK)
+        for half in range(2):
+            gw_ps = ps.tile([P, 2, R], F32, name="gw_ps%d" % half)
+            x_codes, x_scales = xq[half]
+            for i in range(2):
+                rows = slice(i * P, (i + 1) * P)
+                nc.tensor.matmul_mx(out=gw_ps[:, i, :], lhsT=x_codes[:, rows].bitcast(FP8X4),
+                                    lhsT_scale=x_scales[:, rows], rhs=g_codes[:].bitcast(FP8X4),
+                                    rhs_scale=g_scales[:], start=True, stop=True)
+            cols = slice(half * 2 * R, (half + 1) * 2 * R)
+            y = tile("y%d" % half, [P, 2 * R], F32)
+            nc.vector.tensor_tensor(y[:], gw_ps[:].rearrange("p i r -> p (i r)"), old_sb[:, cols], ALU.add)
+            nc.sync.dma_start(out_rows[:, cols], y[:])

@@ -67,8 +67,6 @@ def tile_attend_cratiopairs_w_kernel(tc, tab_words, tab_scales, w1, reserve, wo,
         nc.gpsimd.dma_start(js_sb[:], js.rearrange("o (p t) -> p (o t)", t=PACK))
         nc.vector.memset(placed_a[:], 0.0)
         nc.vector.memset(placed_b[:], 0.0)
-        neg_res = tile("neg_res", [P, 1], F32)
-        nc.gpsimd.tensor_scalar(neg_res[:], res[:], -1.0, 0.0, ALU.mult, ALU.add)
 
         def quantise(name, grouped, width, over=None):
             codes = tile(name + "_codes", [P, width], U32)
@@ -77,36 +75,43 @@ def tile_attend_cratiopairs_w_kernel(tc, tab_words, tab_scales, w1, reserve, wo,
             return codes, scales
 
         tab_codes = tile("tab_codes", [P, J], U16)
-        tab_planes = tile("tab_planes", [P, J], U8)
         w1_il = tile("w1_il", [P, R, PACK], BF16)
         wo_il = tile("wo_il", [P, R, PACK], BF16)
         dy_il = tile("dy_il", [P, M, PACK], BF16)
-        nc.scalar.copy(w1_il[:], w1_raw[:].rearrange("p t r -> p r t"))
-        nc.scalar.copy(wo_il[:], wo_raw[:].rearrange("p t r -> p r t"))
+
+        def interleaved(grouped, raw):
+            return (grouped[:].rearrange("p (c i) t -> p c t i", i=4), raw[:].rearrange("p t (c i) -> p c t i", i=4))
+
+        nc.scalar.copy(*interleaved(w1_il, w1_raw))
+        nc.scalar.copy(*interleaved(wo_il, wo_raw))
         nc.vector.tensor_copy(tab_codes[:], words[:].indirect(slots[:]))
-        nc.vector.tensor_copy(tab_planes[:], planes[:].indirect(slots[:]))
+        tab_planes = [tile("tab_planes0", [P, J // 2], U8), tile("tab_planes1", [P, J // 2], U8, "w1_raw")]
+        nc.vector.tensor_copy(tab_planes[0][:], planes[:].indirect(slots[:, :J // 32]))
         w1_codes, w1_scales = quantise("w1", w1_il[:].rearrange("p r t -> p (r t)"), R)
+        nc.vector.tensor_copy(tab_planes[1][:], planes[:].indirect(slots[:, J // 32:]))
         h1 = tile("h1", [P, J], F32)
         for half in range(2):
             cols = slice(half * J // 2, (half + 1) * J // 2)
             a_ps = ps.tile([P, J // 2], F32, name="a_ps%d" % half)
             nc.tensor.matmul_mx(out=a_ps[:], lhsT=w1_codes[:].bitcast(FP8X4), lhsT_scale=w1_scales[:],
-                                rhs=tab_codes[:, cols].bitcast(FP4X4), rhs_scale=tab_planes[:, cols],
+                                rhs=tab_codes[:, cols].bitcast(FP4X4), rhs_scale=tab_planes[half][:],
                                 start=True, stop=True)
             nc.scalar.activation(h1[:, cols], a_ps[:], ACT.Exp)
 
-        nc.vector.tensor_copy(dy_il[:], dy_raw[:].rearrange("p t m -> p m t"))
+        nc.vector.tensor_copy(*interleaved(dy_il, dy_raw))
         wo_codes, wo_scales = quantise("wo", wo_il[:].rearrange("p r t -> p (r t)"), R)
         dy_codes, dy_scales = quantise("dy", dy_il[:].rearrange("p m t -> p (m t)"), M)
         c0_ps = ps.tile([P, M], F32, name="c0_ps")
         nc.tensor.matmul_mx(out=c0_ps[:], lhsT=wo_codes[:].bitcast(FP8X4), lhsT_scale=wo_scales[:],
                             rhs=dy_codes[:].bitcast(FP8X4), rhs_scale=dy_scales[:], start=True, stop=True)
 
-        x_il = [tile("x_il%d" % half, [P, 2, P, PACK], BF16) for half in range(2)]
 
-        def gather_x(i, over):
+        def gather_x(i, over, pieces=1):
             picked = tile("x_picked%d" % i, [P, J], BF16, over)
-            nc.vector.tensor_copy(picked[:], x_raw[i][:].indirect(slots[:]))
+            n = J // pieces
+            for c in range(pieces):
+                nc.vector.tensor_copy(picked[:, c * n:(c + 1) * n],
+                                      x_raw[i][:].indirect(slots[:, c * n // 16:(c + 1) * n // 16]))
             return picked
 
         def gather_x_on_scalar(i, over):
@@ -116,42 +121,44 @@ def tile_attend_cratiopairs_w_kernel(tc, tab_words, tab_scales, w1, reserve, wo,
             nc.scalar.activation(picked[:], narrow[:].indirect(slots[:]), ACT.Copy)
             return picked
 
+        x_il = [tile("x_il01", [P, 2, P, PACK], BF16), tile("x_il2", [P, 1, P, PACK], BF16),
+                tile("x_il3", [P, 1, P, PACK], BF16)]
+        x_place = [x_il[0][:, 0], x_il[0][:, 1], x_il[1][:, 0], x_il[2][:, 0]]
+
         def turn_x(i, picked):
             pairs = picked[:].bitcast(F32)
             turned = ps.tile([P, 2, P], F32, name="x_turned%d" % (i % 2), tag="x_turned%d" % (i % 2))
             for u in range(2):
                 nc.tensor.transpose(turned[:, u, :], pairs[:, u:J // 2:2], ident[:])
-            nc.scalar.copy(x_il[i // 2][:, i % 2].bitcast(F32), turned[:].rearrange("p u k -> p k u"))
+            nc.scalar.copy(x_place[i].bitcast(F32), turned[:].rearrange("p u k -> p k u"))
 
-        def quantise_x(half, over=None):
-            return quantise("x%d" % half, x_il[half][:].rearrange("p i k t -> p (i k t)"), 2 * P, over)
+        def quantise_x(n, blocks, over=None):
+            return quantise("x%d" % n, x_il[n][:].rearrange("p i k t -> p (i k t)"), blocks * P, over)
 
         root = tile("root", [P, M], F32)
-        nc.scalar.activation(root[:, 0:1], h1[:, J - 1:J], ACT.Abs_reciprocal_sqrt)
         h_a = tile("h_a", [P, M], F32)
         h_b = tile("h_b", [P, M], F32)
         h_sum = tile("h_sum", [P, M], F32)
         top = tile("top", [P, M], F32)
         nc.vector.tensor_copy(h_a[:], h1[:].indirect(firsts[:]))
         nc.vector.tensor_copy(h_b[:], h1[:].indirect(seconds[:]))
-        nc.vector.tensor_tensor(h_sum[:], h_a[:], h_b[:], ALU.add)
         nc.vector.tensor_tensor(top[:], c0_ps[:], h_a[:], ALU.mult)
+        nc.vector.tensor_tensor(h_sum[:], h_a[:], h_b[:], ALU.add)
 
         inv = tile("inv", [P, M], F32)
         nc.scalar.activation(root[:], h_sum[:], ACT.Abs_reciprocal_sqrt, bias=res[:])
         nc.scalar.activation(inv[:], root[:], ACT.Square)
-        neg_rest = tile("neg_rest", [P, M], F32, "h_sum")
-        nc.scalar.activation(neg_rest[:], h_b[:], ACT.Identity, bias=neg_res[:], scale=-1.0)
 
         turn_x(0, gather_x(0, "h1"))
         picked1 = gather_x_on_scalar(1, "root")
 
-        share = tile("share", [P, M], F32, "x_raw0")
-        e2 = tile("e2", [P, M], F32)
-        nc.vector.tensor_tensor(share[:], top[:], inv[:], ALU.mult)
-        nc.vector.scalar_tensor_tensor(e2[:], share[:], -1.0, inv[:], ALU.mult, ALU.mult)
-        nc.vector.tensor_tensor(placed_b[:].indirect(seconds[:]), e2[:], h_b[:], ALU.mult)
-        nc.vector.tensor_tensor(placed_a[:].indirect(firsts[:]), e2[:], neg_rest[:], ALU.mult)
+        over_den = tile("over_den", [P, 3, M], F32, "x_raw0")
+        neg_b, share, rest = over_den[:, 0, :], over_den[:, 1, :], over_den[:, 2, :]
+        nc.vector.scalar_tensor_tensor(neg_b, h_b[:], -1.0, inv[:], ALU.mult, ALU.mult)
+        nc.vector.tensor_tensor(share, top[:], inv[:], ALU.mult)
+        nc.vector.scalar_tensor_tensor(rest, h_b[:], res[:], inv[:], ALU.add, ALU.mult)
+        nc.vector.tensor_tensor(placed_b[:].indirect(seconds[:]), share, neg_b, ALU.mult)
+        nc.vector.tensor_tensor(placed_a[:].indirect(firsts[:]), share, rest, ALU.mult)
 
         da_ps = ps.tile([P, PACK, R], F32, name="da_ps")
 
@@ -161,27 +168,26 @@ def tile_attend_cratiopairs_w_kernel(tc, tab_words, tab_scales, w1, reserve, wo,
                                  start=(first and t == 0), stop=(last and t == PACK - 1))
 
         turn_placed(placed_b, True, False)
-        turn_x(1, picked1)
         turn_placed(placed_a, False, True)
-        turn_x(2, gather_x(2, "h_b"))
-        turn_x(3, gather_x(3, "h_sum"))
+        turn_x(1, picked1)
+        turn_x(2, gather_x(2, "inv"))
+        turn_x(3, gather_x(3, "top"))
         g_il = tile("g_il", [P, R, PACK], BF16, "x_raw3")
         nc.vector.tensor_tensor(g_il[:], da_ps[:].rearrange("p t r -> p r t"),
                                 js_sb[:].unsqueeze(1).to_broadcast([P, R, PACK]), ALU.mult)
-        xq = [quantise_x(0, "js_sb")]
         g_codes, g_scales = quantise("g", g_il[:].rearrange("p r t -> p (r t)"), R)
-        xq.append(quantise_x(1))
+        xq01 = quantise_x(0, 2, "js_sb")
+        stationary = [(xq01, 0), (xq01, P), (quantise_x(1, 1, "top"), 0), (quantise_x(2, 1), 0)]
 
         out_rows = out.rearrange("(p i) r -> p (i r)", i=PACK)
-        for half in range(2):
-            gw_ps = ps.tile([P, 2, R], F32, name="gw_ps%d" % half)
-            x_codes, x_scales = xq[half]
-            for i in range(2):
-                rows = slice(i * P, (i + 1) * P)
-                nc.tensor.matmul_mx(out=gw_ps[:, i, :], lhsT=x_codes[:, rows].bitcast(FP8X4),
-                                    lhsT_scale=x_scales[:, rows], rhs=g_codes[:].bitcast(FP8X4),
+        for first, count in ((0, 3), (3, 1)):
+            gw_ps = ps.tile([P, count, R], F32, name="gw_ps%d" % first)
+            for i in range(count):
+                (x_codes, x_scales), col = stationary[first + i]
+                nc.tensor.matmul_mx(out=gw_ps[:, i, :], lhsT=x_codes[:, col:col + P].bitcast(FP8X4),
+                                    lhsT_scale=x_scales[:, col:col + P], rhs=g_codes[:].bitcast(FP8X4),
                                     rhs_scale=g_scales[:], start=True, stop=True)
-            cols = slice(half * 2 * R, (half + 1) * 2 * R)
-            y = tile("y%d" % half, [P, 2 * R], F32)
+            cols = slice(first * R, (first + count) * R)
+            y = tile("y%d" % first, [P, count * R], F32)
             nc.vector.tensor_tensor(y[:], gw_ps[:].rearrange("p i r -> p (i r)"), old_sb[:, cols], ALU.add)
             nc.sync.dma_start(out_rows[:, cols], y[:])

@@ -49,29 +49,30 @@ def tile_attend_cratiopairs_w_kernel(tc, tab_words, tab_scales, w1, reserve, wo,
 
         nc.vector.memset(planes[:].bitcast(I32), 0)
         nc.sync.dma_start(slots[:], offs)
-        nc.sync.dma_start(firsts[:], offs2)
         nc.sync.dma_start(words[:].bitcast(I32), tab_words[0].bitcast(I32))
         nc.sync.dma_start(w1_raw[:], w1.rearrange("(p t) r -> p t r", t=PACK))
+        nc.sync.dma_start(firsts[:], offs2)
         scale_rows = tab_scales[0].bitcast(I32)
         for q in range(4):
             nc.sync.dma_start(planes[32 * q:32 * q + 4, :].bitcast(I32), scale_rows[4 * q:4 * q + 4, :])
-        nc.sync.dma_start(wo_raw[:], wo.rearrange("(p t) r -> p t r", t=PACK))
         nc.sync.dma_start(dy_raw[:], dy.rearrange("(p t) m -> p t m", t=PACK))
+        nc.sync.dma_start(wo_raw[:], wo.rearrange("(p t) r -> p t r", t=PACK))
         nc.sync.dma_start(seconds[:], offs3)
         x_blocks = xrows.rearrange("(p i) t -> i p t", i=PACK)
         for i in range(PACK):
             nc.sync.dma_start(x_raw[i][:], x_blocks[i])
+        nc.sync.dma_start(js_sb[:], js.rearrange("o (p t) -> p (o t)", t=PACK))
         nc.sync.dma_start(old_sb[:], old.rearrange("(p i) r -> p (i r)", i=PACK))
         make_identity(nc, ident[:])
         nc.gpsimd.dma_start(res[:], reserve)
-        nc.gpsimd.dma_start(js_sb[:], js.rearrange("o (p t) -> p (o t)", t=PACK))
         nc.vector.memset(placed_a[:], 0.0)
         nc.vector.memset(placed_b[:], 0.0)
 
-        def quantise(name, grouped, width, over=None):
+        def quantise(name, grouped, width, scales=None):
             codes = tile(name + "_codes", [P, width], U32)
-            scales = tile(name + "_scales", [P, width], U8, over)
-            nc.vector.quantize_mx(out=codes[:].bitcast(FP8X4), scales=scales[:], in_=grouped)
+            if scales is None:
+                scales = tile(name + "_scales", [P, width], U8)[:]
+            nc.vector.quantize_mx(out=codes[:].bitcast(FP8X4), scales=scales, in_=grouped)
             return codes, scales
 
         tab_codes = tile("tab_codes", [P, J], U16)
@@ -92,7 +93,7 @@ def tile_attend_cratiopairs_w_kernel(tc, tab_words, tab_scales, w1, reserve, wo,
         h1 = tile("h1", [P, J], F32)
         for half in range(2):
             cols = slice(half * J // 2, (half + 1) * J // 2)
-            a_ps = ps.tile([P, J // 2], F32, name="a_ps%d" % half)
+            a_ps = ps.tile([P, J // 2], F32, name="a_ps%d" % half, tag="a_ps%d" % half)
             nc.tensor.matmul_mx(out=a_ps[:], lhsT=w1_codes[:].bitcast(FP8X4), lhsT_scale=w1_scales[:],
                                 rhs=tab_codes[:, cols].bitcast(FP4X4), rhs_scale=tab_planes[half][:],
                                 start=True, stop=True)
@@ -101,7 +102,7 @@ def tile_attend_cratiopairs_w_kernel(tc, tab_words, tab_scales, w1, reserve, wo,
         nc.vector.tensor_copy(*interleaved(dy_il, dy_raw))
         wo_codes, wo_scales = quantise("wo", wo_il[:].rearrange("p r t -> p (r t)"), R)
         dy_codes, dy_scales = quantise("dy", dy_il[:].rearrange("p m t -> p (m t)"), M)
-        c0_ps = ps.tile([P, M], F32, name="c0_ps")
+        c0_ps = ps.tile([P, M], F32, name="c0_ps", tag="c0_ps")
         nc.tensor.matmul_mx(out=c0_ps[:], lhsT=wo_codes[:].bitcast(FP8X4), lhsT_scale=wo_scales[:],
                             rhs=dy_codes[:].bitcast(FP8X4), rhs_scale=dy_scales[:], start=True, stop=True)
 
@@ -127,7 +128,7 @@ def tile_attend_cratiopairs_w_kernel(tc, tab_words, tab_scales, w1, reserve, wo,
 
         def turn_x(i, picked):
             pairs = picked[:].bitcast(F32)
-            turned = ps.tile([P, 2, P], F32, name="x_turned%d" % (i % 2), tag="x_turned%d" % (i % 2))
+            turned = ps.tile([P, 2, P], F32, name="x_turned%d" % i)
             for u in range(2):
                 nc.tensor.transpose(turned[:, u, :], pairs[:, u:J // 2:2], ident[:])
             nc.scalar.copy(x_place[i].bitcast(F32), turned[:].rearrange("p u k -> p k u"))
@@ -172,20 +173,21 @@ def tile_attend_cratiopairs_w_kernel(tc, tab_words, tab_scales, w1, reserve, wo,
         turn_x(1, picked1)
         turn_x(2, gather_x(2, "inv"))
         turn_x(3, gather_x(3, "top"))
-        g_il = tile("g_il", [P, R, PACK], BF16, "x_raw3")
+        g_il = tile("g_il", [P, R, PACK], BF16)
         nc.vector.tensor_tensor(g_il[:], da_ps[:].rearrange("p t r -> p r t"),
                                 js_sb[:].unsqueeze(1).to_broadcast([P, R, PACK]), ALU.mult)
         g_codes, g_scales = quantise("g", g_il[:].rearrange("p r t -> p (r t)"), R)
-        xq01 = quantise_x(0, 2, "js_sb")
-        stationary = [(xq01, 0), (xq01, P), (quantise_x(1, 1, "top"), 0), (quantise_x(2, 1), 0)]
+        x_scales = tile("x_scales", [P, 3 * P], U8, "js_sb")
+        xq01 = quantise_x(0, 2, x_scales[:, :2 * P])
+        stationary = [(xq01, 0), (xq01, P), (quantise_x(1, 1, x_scales[:, 2 * P:]), 0), (quantise_x(2, 1), 0)]
 
         out_rows = out.rearrange("(p i) r -> p (i r)", i=PACK)
-        for first, count in ((0, 3), (3, 1)):
-            gw_ps = ps.tile([P, count, R], F32, name="gw_ps%d" % first)
+        for first, count, bank in ((0, 2, "a_ps0"), (2, 1, "a_ps1"), (3, 1, "c0_ps")):
+            gw_ps = ps.tile([P, count, R], F32, name="gw_ps%d" % first, tag=bank)
             for i in range(count):
-                (x_codes, x_scales), col = stationary[first + i]
+                (x_codes, x_plane), col = stationary[first + i]
                 nc.tensor.matmul_mx(out=gw_ps[:, i, :], lhsT=x_codes[:, col:col + P].bitcast(FP8X4),
-                                    lhsT_scale=x_scales[:, col:col + P], rhs=g_codes[:].bitcast(FP8X4),
+                                    lhsT_scale=x_plane[:, col:col + P], rhs=g_codes[:].bitcast(FP8X4),
                                     rhs_scale=g_scales[:], start=True, stop=True)
             cols = slice(first * R, (first + count) * R)
             y = tile("y%d" % first, [P, count * R], F32)

@@ -55,11 +55,12 @@ def tile_attend_cratiopairs_w_kernel(tc, tab_words, tab_scales, w1, reserve, wo,
         scale_rows = tab_scales[0].bitcast(I32)
         for q in range(4):
             nc.sync.dma_start(planes[32 * q:32 * q + 4, :].bitcast(I32), scale_rows[4 * q:4 * q + 4, :])
+        x_blocks = xrows.rearrange("(p i) t -> i p t", i=PACK)
+        nc.sync.dma_start(x_raw[0][:], x_blocks[0])
         nc.sync.dma_start(dy_raw[:], dy.rearrange("(p t) m -> p t m", t=PACK))
         nc.sync.dma_start(wo_raw[:], wo.rearrange("(p t) r -> p t r", t=PACK))
         nc.sync.dma_start(seconds[:], offs3)
-        x_blocks = xrows.rearrange("(p i) t -> i p t", i=PACK)
-        for i in range(PACK):
+        for i in range(1, PACK):
             nc.sync.dma_start(x_raw[i][:], x_blocks[i])
         nc.sync.dma_start(js_sb[:], js.rearrange("o (p t) -> p (o t)", t=PACK))
         nc.sync.dma_start(old_sb[:], old.rearrange("(p i) r -> p (i r)", i=PACK))
@@ -77,14 +78,12 @@ def tile_attend_cratiopairs_w_kernel(tc, tab_words, tab_scales, w1, reserve, wo,
 
         tab_codes = tile("tab_codes", [P, J], U16)
         w1_il = tile("w1_il", [P, R, PACK], BF16)
-        wo_il = tile("wo_il", [P, R, PACK], BF16)
         dy_il = tile("dy_il", [P, M, PACK], BF16)
 
         def interleaved(grouped, raw):
             return (grouped[:].rearrange("p (c i) t -> p c t i", i=4), raw[:].rearrange("p t (c i) -> p c t i", i=4))
 
         nc.scalar.copy(*interleaved(w1_il, w1_raw))
-        nc.scalar.copy(*interleaved(wo_il, wo_raw))
         nc.vector.tensor_copy(tab_codes[:], words[:].indirect(slots[:]))
         tab_planes = [tile("tab_planes0", [P, J // 2], U8), tile("tab_planes1", [P, J // 2], U8, "w1_raw")]
         nc.vector.tensor_copy(tab_planes[0][:], planes[:].indirect(slots[:, :J // 32]))
@@ -99,64 +98,63 @@ def tile_attend_cratiopairs_w_kernel(tc, tab_words, tab_scales, w1, reserve, wo,
                                 start=True, stop=True)
             nc.scalar.activation(h1[:, cols], a_ps[:], ACT.Exp)
 
-        nc.vector.tensor_copy(*interleaved(dy_il, dy_raw))
-        wo_codes, wo_scales = quantise("wo", wo_il[:].rearrange("p r t -> p (r t)"), R)
-        dy_codes, dy_scales = quantise("dy", dy_il[:].rearrange("p m t -> p (m t)"), M)
-        c0_ps = ps.tile([P, M], F32, name="c0_ps", tag="c0_ps")
-        nc.tensor.matmul_mx(out=c0_ps[:], lhsT=wo_codes[:].bitcast(FP8X4), lhsT_scale=wo_scales[:],
-                            rhs=dy_codes[:].bitcast(FP8X4), rhs_scale=dy_scales[:], start=True, stop=True)
+        nc.scalar.copy(*interleaved(dy_il, dy_raw))
 
-
-        def gather_x(i, over, pieces=1):
-            picked = tile("x_picked%d" % i, [P, J], BF16, over)
-            n = J // pieces
-            for c in range(pieces):
-                nc.vector.tensor_copy(picked[:, c * n:(c + 1) * n],
-                                      x_raw[i][:].indirect(slots[:, c * n // 16:(c + 1) * n // 16]))
+        def gather_x(i):
+            picked = tile("x_picked%d" % i, [P, J], BF16)
+            nc.vector.tensor_copy(picked[:], x_raw[i][:].indirect(slots[:]))
             return picked
 
-        def gather_x_on_scalar(i, over):
-            narrow = tile("x_narrow%d" % i, [P, T], BF16, over)
+        def gather_x_on_scalar(i):
+            narrow = tile("x_narrow%d" % i, [P, T], BF16)
             nc.scalar.activation(narrow[:], x_raw[i][:], ACT.Copy)
             picked = tile("x_picked%d" % i, [P, J], BF16)
             nc.scalar.activation(picked[:], narrow[:].indirect(slots[:]), ACT.Copy)
             return picked
 
-        x_il = [tile("x_il01", [P, 2, P, PACK], BF16), tile("x_il2", [P, 1, P, PACK], BF16),
-                tile("x_il3", [P, 1, P, PACK], BF16)]
-        x_place = [x_il[0][:, 0], x_il[0][:, 1], x_il[1][:, 0], x_il[2][:, 0]]
-
-        def turn_x(i, picked):
+        def turn_x(i, picked, place):
             pairs = picked[:].bitcast(F32)
             turned = ps.tile([P, 2, P], F32, name="x_turned%d" % i)
             for u in range(2):
                 nc.tensor.transpose(turned[:, u, :], pairs[:, u:J // 2:2], ident[:])
-            nc.scalar.copy(x_place[i].bitcast(F32), turned[:].rearrange("p u k -> p k u"))
+            nc.scalar.copy(place.bitcast(F32), turned[:].rearrange("p u k -> p k u"))
 
-        def quantise_x(n, blocks, over=None):
-            return quantise("x%d" % n, x_il[n][:].rearrange("p i k t -> p (i k t)"), blocks * P, over)
+        def quantise_x(name, grouped, scales=None):
+            return quantise(name, grouped[:].rearrange("p i k t -> p (i k t)"), grouped.shape[1] * P, scales)
 
-        root = tile("root", [P, M], F32)
-        h_a = tile("h_a", [P, M], F32)
+        picked0 = gather_x(0)
+        h_a = tile("h_a", [P, M], F32, "x_raw0")
         h_b = tile("h_b", [P, M], F32)
-        h_sum = tile("h_sum", [P, M], F32)
-        top = tile("top", [P, M], F32)
+        h_sum = tile("h_sum", [P, M], F32, "dy_raw")
         nc.vector.tensor_copy(h_a[:], h1[:].indirect(firsts[:]))
         nc.vector.tensor_copy(h_b[:], h1[:].indirect(seconds[:]))
-        nc.vector.tensor_tensor(top[:], c0_ps[:], h_a[:], ALU.mult)
         nc.vector.tensor_tensor(h_sum[:], h_a[:], h_b[:], ALU.add)
 
+        root = tile("root", [P, M], F32)
         inv = tile("inv", [P, M], F32)
         nc.scalar.activation(root[:], h_sum[:], ACT.Abs_reciprocal_sqrt, bias=res[:])
         nc.scalar.activation(inv[:], root[:], ACT.Square)
 
-        turn_x(0, gather_x(0, "h1"))
-        picked1 = gather_x_on_scalar(1, "root")
+        wo_il = tile("wo_il", [P, R, PACK], BF16)
+        nc.vector.tensor_copy(*interleaved(wo_il, wo_raw))
+        dy_codes, dy_scales = quantise("dy", dy_il[:].rearrange("p m t -> p (m t)"), M)
+        wo_codes, wo_scales = quantise("wo", wo_il[:].rearrange("p r t -> p (r t)"), R)
+        c0_ps = ps.tile([P, M], F32, name="c0_ps", tag="c0_ps")
+        nc.tensor.matmul_mx(out=c0_ps[:], lhsT=wo_codes[:].bitcast(FP8X4), lhsT_scale=wo_scales[:],
+                            rhs=dy_codes[:].bitcast(FP8X4), rhs_scale=dy_scales[:], start=True, stop=True)
 
-        over_den = tile("over_den", [P, 3, M], F32, "x_raw0")
-        neg_b, share, rest = over_den[:, 0, :], over_den[:, 1, :], over_den[:, 2, :]
+        x_il01 = tile("x_il01", [P, 2, P, PACK], BF16, "root")
+        x_il2 = tile("x_il2", [P, 1, P, PACK], BF16)
+        x_il3 = tile("x_il3", [P, 1, P, PACK], BF16)
+        turn_x(0, picked0, x_il01[:, 0])
+        turn_x(1, gather_x(1), x_il01[:, 1])
+        picked2 = gather_x_on_scalar(2)
+
+        terms = tile("terms", [P, 4, M], F32, "x_raw1")
+        top, neg_b, share, rest = (terms[:, n, :] for n in range(4))
+        nc.vector.tensor_tensor(top, c0_ps[:], h_a[:], ALU.mult)
         nc.vector.scalar_tensor_tensor(neg_b, h_b[:], -1.0, inv[:], ALU.mult, ALU.mult)
-        nc.vector.tensor_tensor(share, top[:], inv[:], ALU.mult)
+        nc.vector.tensor_tensor(share, top, inv[:], ALU.mult)
         nc.vector.scalar_tensor_tensor(rest, h_b[:], res[:], inv[:], ALU.add, ALU.mult)
         nc.vector.tensor_tensor(placed_b[:].indirect(seconds[:]), share, neg_b, ALU.mult)
         nc.vector.tensor_tensor(placed_a[:].indirect(firsts[:]), share, rest, ALU.mult)
@@ -170,16 +168,15 @@ def tile_attend_cratiopairs_w_kernel(tc, tab_words, tab_scales, w1, reserve, wo,
 
         turn_placed(placed_b, True, False)
         turn_placed(placed_a, False, True)
-        turn_x(1, picked1)
-        turn_x(2, gather_x(2, "inv"))
-        turn_x(3, gather_x(3, "top"))
+        turn_x(2, picked2, x_il2[:, 0])
+        turn_x(3, gather_x(3), x_il3[:, 0])
         g_il = tile("g_il", [P, R, PACK], BF16)
         nc.vector.tensor_tensor(g_il[:], da_ps[:].rearrange("p t r -> p r t"),
                                 js_sb[:].unsqueeze(1).to_broadcast([P, R, PACK]), ALU.mult)
+        xq01 = quantise_x("x01", x_il01, tile("x01_scales", [P, 2 * P], U8, "x_raw3")[:])
         g_codes, g_scales = quantise("g", g_il[:].rearrange("p r t -> p (r t)"), R)
-        x_scales = tile("x_scales", [P, 3 * P], U8, "js_sb")
-        xq01 = quantise_x(0, 2, x_scales[:, :2 * P])
-        stationary = [(xq01, 0), (xq01, P), (quantise_x(1, 1, x_scales[:, 2 * P:]), 0), (quantise_x(2, 1), 0)]
+        xq2 = quantise_x("x2", x_il2, tile("x2_scales", [P, P], U8, "js_sb")[:])
+        stationary = [(xq01, 0), (xq01, P), (xq2, 0), (quantise_x("x3", x_il3), 0)]
 
         out_rows = out.rearrange("(p i) r -> p (i r)", i=PACK)
         for first, count, bank in ((0, 2, "a_ps0"), (2, 1, "a_ps1"), (3, 1, "c0_ps")):

from contextlib import ExitStack

import concourse.mybir as mybir
from concourse.masks import make_identity

K, R, F, T, J, M = 512, 128, 512, 2048, 512, 256
FLOPS = 2 * K * R * J + 2 * F * R * M + 2 * J * K * R

F32 = mybir.dt.float32
BF16 = mybir.dt.bfloat16
I32 = mybir.dt.int32
U32 = mybir.dt.uint32
U16 = mybir.dt.uint16
U8 = mybir.dt.uint8
FP8X4 = mybir.dt.float8_e4m3fn_x4
FP4X4 = mybir.dt.float4_e2m1fn_x4
ALU = mybir.AluOpType
ACT = mybir.ActivationFunctionType

P = 128
PACK = 4


def tile_attend_cratiopairs_w_kernel(tc, tab_words, tab_scales, w1, reserve, wo, dy, js, xrows, old,
                                      offs, offs2, offs3, out):
    nc = tc.nc
    with ExitStack() as ctx:
        sb = ctx.enter_context(tc.tile_pool(name="sb", bufs=1))
        ps = ctx.enter_context(tc.psum_pool(name="ps", bufs=1))

        def tile(name, shape, dtype, over=None):
            return sb.tile(shape, dtype, name=name, tag=over or name, align_bytes=64)

        slots = sb.tile([P, J // 16], U16, name="slots")
        firsts = sb.tile([P, M // 16], U16, name="firsts")
        seconds = sb.tile([P, M // 16], U16, name="seconds")
        words = tile("words", [P, T], U16)
        planes = tile("planes", [P, T], U8)
        w1_raw = tile("w1_raw", [P, PACK, R], F32)
        wo_raw = tile("wo_raw", [P, PACK, R], F32)
        dy_raw = tile("dy_raw", [P, PACK, M], F32)
        x_raw = [tile("x_raw%d" % i, [P, T], F32) for i in range(PACK)]
        old_sb = tile("old_sb", [P, PACK * R], F32)
        res = tile("res", [P, 1], F32)
        js_sb = tile("js_sb", [P, PACK], F32)
        ident = tile("ident", [P, P], F32)
        placed_a = tile("placed_a", [P, J], F32)
        placed_b = tile("placed_b", [P, J], F32)

        nc.vector.memset(planes[:].bitcast(I32), 0)
        nc.sync.dma_start(slots[:], offs)
        nc.sync.dma_start(words[:].bitcast(I32), tab_words[0].bitcast(I32))
        nc.sync.dma_start(w1_raw[:], w1.rearrange("(p t) r -> p t r", t=PACK))
        nc.sync.dma_start(firsts[:], offs2)
        scale_rows = tab_scales[0].bitcast(I32)
        for q in range(4):
            nc.sync.dma_start(planes[32 * q:32 * q + 4, :].bitcast(I32), scale_rows[4 * q:4 * q + 4, :])
        x_blocks = xrows.rearrange("(p i) t -> i p t", i=PACK)
        nc.sync.dma_start(x_raw[0][:], x_blocks[0])
        nc.sync.dma_start(dy_raw[:], dy.rearrange("(p t) m -> p t m", t=PACK))
        nc.sync.dma_start(wo_raw[:], wo.rearrange("(p t) r -> p t r", t=PACK))
        nc.sync.dma_start(seconds[:], offs3)
        for i in range(1, PACK):
            nc.sync.dma_start(x_raw[i][:], x_blocks[i])
        nc.sync.dma_start(js_sb[:], js.rearrange("o (p t) -> p (o t)", t=PACK))
        nc.sync.dma_start(old_sb[:], old.rearrange("(p i) r -> p (i r)", i=PACK))
        make_identity(nc, ident[:])
        nc.gpsimd.dma_start(res[:], reserve)
        nc.vector.memset(placed_a[:], 0.0)
        nc.vector.memset(placed_b[:], 0.0)

        def quantise(name, grouped, width, scales=None):
            codes = tile(name + "_codes", [P, width], U32)
            if scales is None:
                scales = tile(name + "_scales", [P, width], U8)[:]
            nc.vector.quantize_mx(out=codes[:].bitcast(FP8X4), scales=scales, in_=grouped)
            return codes, scales

        tab_codes = tile("tab_codes", [P, J], U16)
        w1_il = tile("w1_il", [P, R, PACK], BF16)
        dy_il = tile("dy_il", [P, M, PACK], BF16)

        def interleaved(grouped, raw):
            return (grouped[:].rearrange("p (c i) t -> p c t i", i=4), raw[:].rearrange("p t (c i) -> p c t i", i=4))

        nc.scalar.copy(*interleaved(w1_il, w1_raw))
        nc.vector.tensor_copy(tab_codes[:], words[:].indirect(slots[:]))
        tab_planes = [tile("tab_planes0", [P, J // 2], U8), tile("tab_planes1", [P, J // 2], U8, "w1_raw")]
        nc.vector.tensor_copy(tab_planes[0][:], planes[:].indirect(slots[:, :J // 32]))
        w1_codes, w1_scales = quantise("w1", w1_il[:].rearrange("p r t -> p (r t)"), R)
        nc.vector.tensor_copy(tab_planes[1][:], planes[:].indirect(slots[:, J // 32:]))
        h1 = tile("h1", [P, J], F32)
        for half in range(2):
            cols = slice(half * J // 2, (half + 1) * J // 2)
            a_ps = ps.tile([P, J // 2], F32, name="a_ps%d" % half, tag="a_ps%d" % half)
            nc.tensor.matmul_mx(out=a_ps[:], lhsT=w1_codes[:].bitcast(FP8X4), lhsT_scale=w1_scales[:],
                                rhs=tab_codes[:, cols].bitcast(FP4X4), rhs_scale=tab_planes[half][:],
                                start=True, stop=True)
            nc.scalar.activation(h1[:, cols], a_ps[:], ACT.Exp)

        nc.scalar.copy(*interleaved(dy_il, dy_raw))

        def gather_x(i):
            picked = tile("x_picked%d" % i, [P, J], BF16)
            nc.vector.tensor_copy(picked[:], x_raw[i][:].indirect(slots[:]))
            return picked

        def gather_x_on_scalar(i):
            narrow = tile("x_narrow%d" % i, [P, T], BF16)
            nc.scalar.activation(narrow[:], x_raw[i][:], ACT.Copy)
            picked = tile("x_picked%d" % i, [P, J], BF16)
            nc.scalar.activation(picked[:], narrow[:].indirect(slots[:]), ACT.Copy)
            return picked

        def turn_x(i, picked, place):
            pairs = picked[:].bitcast(F32)
            turned = ps.tile([P, 2, P], F32, name="x_turned%d" % i)
            for u in range(2):
                nc.tensor.transpose(turned[:, u, :], pairs[:, u:J // 2:2], ident[:])
            nc.scalar.copy(place.bitcast(F32), turned[:].rearrange("p u k -> p k u"))

        def quantise_x(name, grouped, scales=None):
            return quantise(name, grouped[:].rearrange("p i k t -> p (i k t)"), grouped.shape[1] * P, scales)

        picked0 = gather_x(0)
        h_a = tile("h_a", [P, M], F32, "x_raw0")
        h_b = tile("h_b", [P, M], F32)
        h_sum = tile("h_sum", [P, M], F32, "dy_raw")
        nc.vector.tensor_copy(h_a[:], h1[:].indirect(firsts[:]))
        nc.vector.tensor_copy(h_b[:], h1[:].indirect(seconds[:]))
        nc.vector.tensor_tensor(h_sum[:], h_a[:], h_b[:], ALU.add)

        root = tile("root", [P, M], F32)
        inv = tile("inv", [P, M], F32)
        nc.scalar.activation(root[:], h_sum[:], ACT.Abs_reciprocal_sqrt, bias=res[:])
        nc.scalar.activation(inv[:], root[:], ACT.Square)

        wo_il = tile("wo_il", [P, R, PACK], BF16)
        nc.vector.tensor_copy(*interleaved(wo_il, wo_raw))
        dy_codes, dy_scales = quantise("dy", dy_il[:].rearrange("p m t -> p (m t)"), M)
        wo_codes, wo_scales = quantise("wo", wo_il[:].rearrange("p r t -> p (r t)"), R)
        c0_ps = ps.tile([P, M], F32, name="c0_ps", tag="c0_ps")
        nc.tensor.matmul_mx(out=c0_ps[:], lhsT=wo_codes[:].bitcast(FP8X4), lhsT_scale=wo_scales[:],
                            rhs=dy_codes[:].bitcast(FP8X4), rhs_scale=dy_scales[:], start=True, stop=True)

        x_il01 = tile("x_il01", [P, 2, P, PACK], BF16, "root")
        x_il2 = tile("x_il2", [P, 1, P, PACK], BF16)
        x_il3 = tile("x_il3", [P, 1, P, PACK], BF16)
        turn_x(0, picked0, x_il01[:, 0])
        turn_x(1, gather_x(1), x_il01[:, 1])
        picked2 = gather_x_on_scalar(2)

        terms = tile("terms", [P, 4, M], F32, "x_raw1")
        top, neg_b, share, rest = (terms[:, n, :] for n in range(4))
        nc.vector.tensor_tensor(top, c0_ps[:], h_a[:], ALU.mult)
        nc.vector.scalar_tensor_tensor(neg_b, h_b[:], -1.0, inv[:], ALU.mult, ALU.mult)
        nc.vector.tensor_tensor(share, top, inv[:], ALU.mult)
        nc.vector.scalar_tensor_tensor(rest, h_b[:], res[:], inv[:], ALU.add, ALU.mult)
        nc.vector.tensor_tensor(placed_b[:].indirect(seconds[:]), share, neg_b, ALU.mult)
        nc.vector.tensor_tensor(placed_a[:].indirect(firsts[:]), share, rest, ALU.mult)

        da_ps = ps.tile([P, PACK, R], F32, name="da_ps")

        def turn_placed(placed, first, last):
            for t in range(PACK):
                nc.tensor.matmul(da_ps[:, t, :], lhsT=placed[:, t:J:PACK], rhs=ident[:], is_transpose=True,
                                 start=(first and t == 0), stop=(last and t == PACK - 1))

        turn_placed(placed_b, True, False)
        turn_placed(placed_a, False, True)
        turn_x(2, picked2, x_il2[:, 0])
        turn_x(3, gather_x(3), x_il3[:, 0])
        g_il = tile("g_il", [P, R, PACK], BF16)
        nc.vector.tensor_tensor(g_il[:], da_ps[:].rearrange("p t r -> p r t"),
                                js_sb[:].unsqueeze(1).to_broadcast([P, R, PACK]), ALU.mult)
        xq01 = quantise_x("x01", x_il01, tile("x01_scales", [P, 2 * P], U8, "x_raw3")[:])
        g_codes, g_scales = quantise("g", g_il[:].rearrange("p r t -> p (r t)"), R)
        xq2 = quantise_x("x2", x_il2, tile("x2_scales", [P, P], U8, "js_sb")[:])
        stationary = [(xq01, 0), (xq01, P), (xq2, 0), (quantise_x("x3", x_il3), 0)]

        out_rows = out.rearrange("(p i) r -> p (i r)", i=PACK)
        for first, count, bank in ((0, 2, "a_ps0"), (2, 1, "a_ps1"), (3, 1, "c0_ps")):
            gw_ps = ps.tile([P, count, R], F32, name="gw_ps%d" % first, tag=bank)
            for i in range(count):
                (x_codes, x_plane), col = stationary[first + i]
                nc.tensor.matmul_mx(out=gw_ps[:, i, :], lhsT=x_codes[:, col:col + P].bitcast(FP8X4),
                                    lhsT_scale=x_plane[:, col:col + P], rhs=g_codes[:].bitcast(FP8X4),
                                    rhs_scale=g_scales[:], start=True, stop=True)
            cols = slice(first * R, (first + count) * R)
            y = tile("y%d" % first, [P, count * R], F32)
            nc.vector.tensor_tensor(y[:], gw_ps[:].rearrange("p i r -> p (i r)"), old_sb[:, cols], ALU.add)
            nc.sync.dma_start(out_rows[:, cols], y[:])
